import numpy as np
import ml_dtypes


def mxq(x, axis, fmt="e4m3"):
    dtype, down = {"e4m3": (ml_dtypes.float8_e4m3fn, 7), "e5m2": (ml_dtypes.float8_e5m2, 14)}[fmt]
    v = np.moveaxis(np.asarray(x, np.float32).astype(ml_dtypes.bfloat16).astype(np.float64), axis, -1)
    blocks = v.reshape(v.shape[:-1] + (-1, 32))
    amax = np.abs(blocks).max(-1, keepdims=True)
    byte = np.maximum(np.where(amax > 0, np.frexp(amax)[1] - 1 + 127, 0) - down, 1)
    scale = np.exp2(byte - 127.0)
    codes = (blocks / scale).astype(np.float32).astype(dtype).astype(np.float64)
    return np.moveaxis((codes * scale).reshape(v.shape), -1, axis)


WIDE = False


def mx_kscale(k):
    if not WIDE:
        return np.ones(k)
    levels = np.array([10, -10, 5, -5, 0])
    if k % 512:
        return np.exp2(np.random.permutation(np.resize(levels, k // 32))).repeat(32)
    a = np.empty((k // 512, 16))
    for p in range(k // 512):
        a[p, :8] = np.random.permutation(np.resize(levels, 8))
        for g in range(8):
            far = levels[np.abs(levels - a[p, g]) >= 10]
            a[p, g + 8] = far[np.random.randint(len(far))]
    return np.exp2(a.ravel()).repeat(32)


def f64(x):
    return np.asarray(x).astype(np.float64)


def striped(idx):
    return np.tile(idx.reshape(-1, 16).T, (8, 1)).astype(np.uint16)


def unstriped(offs):
    return offs[:16].T.reshape(-1).astype(np.int64)


def striped8(idx):
    return np.concatenate([x.reshape(-1, 16).T for x in idx]).astype(np.uint16)


def runs(offs, k):
    lists = np.stack([offs[16 * r : 16 * r + 16].T.reshape(-1) for r in range(8)]).astype(np.int64)
    return lists[np.arange(k) % 512 // 64]


def pack_weight(w):
    k, n = w.shape
    w = f64(np.asarray(w, np.float32).astype(ml_dtypes.bfloat16)).reshape(k // 32, 32, n)
    amax = np.abs(w).max(1)
    byte = np.clip(np.where(amax > 0, np.frexp(amax)[1] - 1 + 127 - 7, 1), 1, 254)
    scaled = (w * np.exp2(127.0 - byte)[:, None, :]).reshape(k, n).astype(np.float32)
    words = np.ascontiguousarray(scaled.reshape(k // 512, 128, 4, n).transpose(0, 1, 3, 2)).astype(ml_dtypes.float8_e4m3fn).view(np.uint8)
    return words, np.ascontiguousarray(byte.astype(np.uint8).reshape(k // 512, 16, n))


def unpack_weight(words, scales):
    g, p, n, _ = words.shape
    vals = np.ascontiguousarray(words).view(ml_dtypes.float8_e4m3fn).astype(np.float64) * np.repeat(np.exp2(scales.astype(np.float64) - 127.0), 8, axis=1)[..., None]
    return vals.transpose(0, 1, 3, 2).reshape(g * 512, n)

def planes(y):
    n, m = y.shape
    v = y.astype(np.float32).astype(ml_dtypes.bfloat16).astype(np.float64).reshape(n // 32, 32, m)
    top = np.abs(v).max(1)
    byte = np.clip(np.where(top > 0, np.frexp(top)[1] - 1 + 127 - 7, 1), 1, 254)
    codes = (v * np.exp2(127.0 - byte)[:, None, :]).reshape(n, m).astype(np.float32).astype(ml_dtypes.float8_e4m3fn).view(np.uint8)
    words = codes.reshape(n // 512, 128, 4, m).transpose(0, 1, 3, 2)
    return np.ascontiguousarray(words), np.ascontiguousarray(byte.astype(np.uint8).reshape(n // 512, 16, m))


K, T, S, N, H = 512, 2048, 512, 512, 512


def setup_inputs():
    n = np.random.standard_normal
    s = mx_kscale(K)[:, None]
    u = mx_kscale(H)
    packed_xT = pack_weight(n((K, T)) * s)
    packed_w1 = pack_weight(n((K, H)) / np.sqrt(K) / s)
    packed_w2 = pack_weight(n((K, H)) / np.sqrt(K) / s)
    packed_w3 = pack_weight(n((H, N)) / np.sqrt(2 * H) / u[:, None])
    packed_w4 = pack_weight(n((H, N)) / np.sqrt(2 * H) / u[:, None])
    return {
        "x_words": packed_xT[0],
        "x_scales": packed_xT[1],
        "w1_words": packed_w1[0],
        "w1_scales": packed_w1[1],
        "w2_words": packed_w2[0],
        "w2_scales": packed_w2[1],
        "gn": (np.random.uniform(0.5, 1.5, (H, 1)) * u[:, None]).astype(np.float32),
        "gm": (np.random.uniform(0.5, 1.5, (H, 1)) * u[:, None]).astype(np.float32),
        "w3_words": packed_w3[0],
        "w3_scales": packed_w3[1],
        "w4_words": packed_w4[0],
        "w4_scales": packed_w4[1],
        "offs": striped(np.random.permutation(T)[:S]),
        "hz": striped8(np.random.randint(0, T, (8, S))),
        "n1": striped(np.random.permutation(S)),
        "n2": striped(np.random.permutation(S)),
        "n3": striped(np.random.permutation(S)),
        "n4": striped(np.random.permutation(S)),
        "n5": striped(np.random.permutation(S)),
    }


def reference(x_words, x_scales, w1_words, w1_scales, w2_words, w2_scales, gn, gm, w3_words, w3_scales, w4_words, w4_scales, offs, hz, n1, n2, n3, n4, n5):
    xq = unpack_weight(x_words, x_scales)[:, unstriped(offs)]
    y = unpack_weight(w1_words, w1_scales).T @ xq
    pa = y[:, unstriped(n1)]
    z = f64(gn) * ((2.0 * (y * pa)) / ((y) ** 2 + (pa) ** 2 + 0.5))
    x_hz = unpack_weight(x_words, x_scales)[np.arange(K)[:, None], runs(hz, K)]
    d = unpack_weight(w2_words, w2_scales).T @ x_hz
    z2 = f64(gm) * (d / (np.abs(d[:, unstriped(n2)]) + 0.5))
    h = unpack_weight(w3_words, w3_scales).T @ mxq(z, 0, "e4m3") + unpack_weight(w4_words, w4_scales).T @ mxq(z2, 0, "e4m3")
    out_0 = 0.75 * (h * h[:, unstriped(n3)] + h[:, unstriped(n4)] * h[:, unstriped(n5)])
    return (out_0,) + planes(out_0)

@@ -1,0 +1,281 @@
+from contextlib import ExitStack
+
+import concourse.mybir as mybir
+
+K, T, S, N, H = 512, 2048, 512, 512, 512
+FLOPS = 4 * 2 * 512 * 512 * 512
+
+F32 = mybir.dt.float32
+BF16 = mybir.dt.bfloat16
+I32 = mybir.dt.int32
+U32 = mybir.dt.uint32
+U16 = mybir.dt.uint16
+U8 = mybir.dt.uint8
+FP8X4 = mybir.dt.float8_e4m3fn_x4
+ACT = mybir.ActivationFunctionType
+ALU = mybir.AluOpType
+
+P = 128
+PACK = 4
+HALF = S // 2
+QUARTER = S // 4
+OUT_CHUNKS = (128, 128, 128, 128)
+N2_ON_VECTOR = (1, 1)
+N3_ON_SCALAR = ((0, 0),)
+
+
+def tile_picked_hjoinharmnormdot_none_po_kernel(
+    tc, x_words, x_scales, w1_words, w1_scales, w2_words, w2_scales, gn, gm,
+    w3_words, w3_scales, w4_words, w4_scales, offs, hz, n1, n2, n3, n4, n5,
+    out_0, out_1, out_2,
+):
+    nc = tc.nc
+
+    with ExitStack() as ctx:
+        keep = ctx.enter_context(tc.tile_pool(name="keep", bufs=1))
+        psum = ctx.enter_context(tc.psum_pool(name="psum", bufs=1))
+
+        def sb(name, shape, dtype):
+            return keep.tile(shape, dtype, name=name, align_bytes=64)
+
+        def load_list(name, src):
+            tile = keep.tile([P, S // 16], U16, name=name)
+            nc.sync.dma_start(tile[:], src)
+            return tile
+
+        def entries(lst, start, count):
+            return lst[:, start // 16 : (start + count) // 16]
+
+        def load_words(tile, src):
+            nc.sync.dma_start(tile[:], src[0].rearrange("p n t -> p (n t)").bitcast(I32))
+
+        def load_scale_rows(tile, src, first):
+            for q in range(4):
+                nc.sync.dma_start(
+                    tile[32 * q + first : 32 * q + first + 4, :].bitcast(I32),
+                    src[0, 4 * q : 4 * q + 4, :].bitcast(I32),
+                )
+
+        def deal(name, raw, dtype, view):
+            tile = sb(name, [P, H], dtype)
+            nc.vector.tensor_copy(
+                tile[:].bitcast(view).rearrange("p (t m) -> p m t", t=PACK),
+                raw[:].bitcast(view).rearrange("p (m t) -> p m t", t=PACK),
+            )
+            return tile
+
+        def place_scale_rows(dst, picked):
+            for r in range(4):
+                nc.sync.dma_start(dst[r:P:32, :].bitcast(I32), picked[8 * r : P : 32, :].bitcast(I32))
+
+        def woven(ap):
+            return ap.rearrange("p (c i) t -> p c t i", i=4)
+
+        def planar(ap):
+            return ap.rearrange("p t (c i) -> p c t i", i=4)
+
+        xs_rows = sb("xs_rows", [P, T], U8)
+        xs_runs = sb("xs_runs", [P, T], U8)
+        ws_raw = sb("ws_raw", [P, H], U8)
+        ws2_raw = sb("ws2_raw", [P, H], U8)
+        xs_hz = sb("xs_hz", [P, S], U8)
+        nc.gpsimd.memset(ws_raw[:].bitcast(I32), 0)
+        nc.vector.memset(xs_rows[:, : T // 2].bitcast(I32), 0)
+        nc.gpsimd.memset(xs_rows[:, T // 2 :].bitcast(I32), 0)
+        for tile in (xs_runs, ws2_raw, xs_hz):
+            nc.gpsimd.memset(tile[:].bitcast(I32), 0)
+        quarter = sb("quarter", [P, 1], F32)
+        half = sb("half", [P, 1], F32)
+        nc.gpsimd.memset(quarter[:], 0.25)
+        nc.gpsimd.memset(half[:], 0.5)
+
+        xw_table = sb("xw_table", [P, T], I32)
+        wa_raw = sb("wa_raw", [P, H], I32)
+        wb_raw = sb("wb_raw", [P, H], I32)
+        gn_t = sb("gn_t", [P, PACK], F32)
+        gm_t = sb("gm_t", [P, PACK], F32)
+        offs_t = load_list("offs_t", offs)
+        load_words(xw_table, x_words)
+        load_words(wa_raw, w1_words)
+        load_scale_rows(xs_rows, x_scales, 0)
+        load_scale_rows(ws_raw, w1_scales, 0)
+        n1_t = load_list("n1_t", n1)
+        nc.sync.dma_start(xs_runs[0:P:8, :].bitcast(I32), x_scales[0].bitcast(I32))
+        hz_t = load_list("hz_t", hz)
+        load_words(wb_raw, w2_words)
+        load_scale_rows(ws2_raw, w2_scales, 0)
+        nc.sync.dma_start(gn_t[:], gn.rearrange("(p t) o -> p (t o)", t=PACK))
+        nc.sync.dma_start(gm_t[:], gm.rearrange("(p t) o -> p (t o)", t=PACK))
+        n2_t = load_list("n2_t", n2)
+        n3_t = load_list("n3_t", n3)
+        n4_t = load_list("n4_t", n4)
+        n5_t = load_list("n5_t", n5)
+
+        xs_offs = sb("xs_offs", [P, S], U8)
+        nc.vector.tensor_copy(xs_offs[:], xs_rows[:].indirect(offs_t[:]))
+        w1_t = deal("w1_t", wa_raw, I32, U32)
+        ws1 = deal("ws1", ws_raw, U8, U8)
+
+        xw_offs = sb("xw_offs", [P, S], I32)
+        nc.vector.tensor_copy(xw_offs[:].bitcast(U32), xw_table[:].bitcast(U32).indirect(offs_t[:]))
+        y_ps = [psum.tile([P, S], F32, name=f"y_ps{t}", tag=f"rows{t}") for t in range(PACK)]
+        for t in range(PACK):
+            m = slice(P * t, P * (t + 1))
+            nc.tensor.matmul_mx(
+                out=y_ps[t][:], lhsT=w1_t[:, m].bitcast(FP8X4), lhsT_scale=ws1[:, m],
+                rhs=xw_offs[:].bitcast(FP8X4), rhs_scale=xs_offs[:], start=True, stop=True,
+            )
+
+        picked_hz = sb("picked_hz", [P, S], U8)
+        nc.vector.tensor_copy(picked_hz[:], xs_runs[:].indirect(hz_t[:]))
+        place_scale_rows(xs_hz, picked_hz)
+        xw_hz = sb("xw_hz", [P, S], I32)
+        nc.vector.tensor_copy(xw_hz[:].bitcast(U32), xw_table[:].bitcast(U32).indirect(hz_t[:]))
+        def columns(j):
+            return slice(QUARTER * j, QUARTER * (j + 1))
+
+        y_sb = [sb(f"y_sb{t}", [P, S], F32) for t in range(PACK)]
+        y_sq = sb("y_sq", [P, PACK, S], F32)
+        pa = sb("pa", [P, PACK, S], F32)
+        pa_sq = sb("pa_sq", [P, PACK, S], F32)
+        squares = sb("squares", [P, PACK, S], F32)
+        root = sb("root", [P, PACK, S], F32)
+        numer = sb("numer", [P, PACK, S], F32)
+        inverse = sb("inverse", [P, PACK, S], F32)
+        z_bf = sb("z_bf", [P, S, PACK], BF16)
+        z_words = sb("z_words", [P, S], U32)
+        z_scales = sb("z_scales", [P, S], U8)
+        d_abs = [sb(f"d_abs{j}", [P, S], F32) for j in range(4)]
+        d_root = sb("d_root", [P, 4, PACK, QUARTER], F32)
+        gain_over = [sb(f"gain_over{t}", [P, S], F32) for t in range(PACK)]
+        looked = sb("looked", [P, PACK, S], F32)
+        z2_bf = sb("z2_bf", [P, S, PACK], BF16)
+        z2_words = sb("z2_words", [P, S], U32)
+        z2_scales = sb("z2_scales", [P, S], U8)
+
+        def quantise(words, scales, values, cols):
+            nc.vector.quantize_mx(
+                out=words[:, cols].bitcast(FP8X4), scales=scales[:, cols],
+                in_=values[:, cols, :].rearrange("p c t -> p (c t)"),
+            )
+
+        def fetch(on_scalar, dst, window, lst, start, count):
+            picked = window[:].indirect(entries(lst, start, count))
+            if on_scalar:
+                nc.scalar.activation(dst, picked, ACT.Copy)
+            else:
+                nc.vector.tensor_copy(dst, picked)
+
+        for t in range(PACK):
+            nc.scalar.activation(y_sb[t][:], y_ps[t][:], ACT.Copy)
+
+        w2_t = deal("w2_t", wb_raw, I32, U32)
+        ws2 = deal("ws2", ws2_raw, U8, U8)
+        load_words(wa_raw, w3_words)
+        load_words(wb_raw, w4_words)
+        load_scale_rows(ws_raw, w3_scales, 4)
+        load_scale_rows(ws_raw, w4_scales, 8)
+        d_ps = [psum.tile([P, PACK, QUARTER], F32, name=f"d_ps{j}", tag=f"cols{j}") for j in range(4)]
+        for j in range(4):
+            for t in range(PACK):
+                m = slice(P * t, P * (t + 1))
+                nc.tensor.matmul_mx(
+                    out=d_ps[j][:, t, :], lhsT=w2_t[:, m].bitcast(FP8X4), lhsT_scale=ws2[:, m],
+                    rhs=xw_hz[:, columns(j)].bitcast(FP8X4), rhs_scale=xs_hz[:, columns(j)], start=True, stop=True,
+                )
+
+        for t in range(PACK):
+            nc.scalar.activation(y_sq[:, t, :], y_ps[t][:], ACT.Square)
+            for start in (0, HALF):
+                fetch(False, pa[:, t, start : start + HALF], y_sb[t], n1_t, start, HALF)
+        for j in range(4):
+            nc.scalar.activation(d_abs[j][:], d_ps[j][:].rearrange("p t c -> p (t c)"), ACT.Abs)
+        for j in range(4):
+            nc.scalar.activation(
+                d_root[:, j, :, :].rearrange("p t c -> p (t c)"), d_abs[j][:],
+                ACT.Abs_reciprocal_sqrt, bias=half[:], scale=1.0,
+            )
+        for t in range(PACK):
+            nc.vector.scalar_tensor_tensor(numer[:, t, :], y_ps[t][:], gn_t[:, t : t + 1], pa[:, t, :], ALU.mult, ALU.mult)
+        for t in range(PACK):
+            nc.vector.scalar_tensor_tensor(
+                gain_over[t][:].rearrange("p (j c) -> p j c", j=4), d_root[:, :, t, :], gm_t[:, t : t + 1],
+                d_root[:, :, t, :], ALU.mult, ALU.mult,
+            )
+        for t in range(PACK):
+            nc.scalar.activation(pa_sq[:, t, :], pa[:, t, :], ACT.Square)
+            nc.vector.tensor_tensor(squares[:, t, :], y_sq[:, t, :], pa_sq[:, t, :], ALU.add)
+        w3_t = deal("w3_t", wa_raw, I32, U32)
+        w4_t = deal("w4_t", wb_raw, I32, U32)
+        ws34 = deal("ws34", ws_raw, U8, U8)
+
+        for start in (0, HALF):
+            for t in range(PACK):
+                fetch(t >= N2_ON_VECTOR[start // HALF], looked[:, t, start : start + HALF], gain_over[t], n2_t, start, HALF)
+            for j in (start // QUARTER, start // QUARTER + 1):
+                nc.vector.tensor_tensor(
+                    woven(z2_bf[:, columns(j), :]), planar(d_ps[j][:]), planar(looked[:, :, columns(j)]), ALU.mult
+                )
+            quantise(z2_words, z2_scales, z2_bf, slice(start, start + HALF))
+
+        h_ps = [psum.tile([P, S], F32, name=f"h_ps{t}", tag=f"rows{t}") for t in range(PACK)]
+        for t in range(PACK):
+            m = slice(P * t, P * (t + 1))
+            nc.tensor.matmul_mx(
+                out=h_ps[t][:], lhsT=w4_t[:, m].bitcast(FP8X4), lhsT_scale=ws34[8:P, m],
+                rhs=z2_words[:].bitcast(FP8X4), rhs_scale=z2_scales[:], start=True, stop=False,
+            )
+
+        for j in range(4):
+            cols = columns(j)
+            nc.scalar.activation(root[:, :, cols], squares[:, :, cols], ACT.Abs_reciprocal_sqrt, bias=quarter[:], scale=0.5)
+            nc.scalar.activation(inverse[:, :, cols], root[:, :, cols], ACT.Square)
+            nc.vector.tensor_tensor(woven(z_bf[:, cols, :]), planar(numer[:, :, cols]), planar(inverse[:, :, cols]), ALU.mult)
+            quantise(z_words, z_scales, z_bf, cols)
+
+        for t in range(PACK):
+            m = slice(P * t, P * (t + 1))
+            nc.tensor.matmul_mx(
+                out=h_ps[t][:], lhsT=w3_t[:, m].bitcast(FP8X4), lhsT_scale=ws34[4:P, m],
+                rhs=z_words[:].bitcast(FP8X4), rhs_scale=z_scales[:], start=False, stop=True,
+            )
+
+        h_sb = [sb(f"h_sb{t}", [P, S], F32) for t in range(PACK)]
+        for t in range(PACK):
+            if t % 2 == 0:
+                nc.scalar.activation(h_sb[t][:], h_ps[t][:], ACT.Copy)
+            else:
+                nc.vector.tensor_copy(h_sb[t][:], h_ps[t][:])
+
+        out_rows = out_0.rearrange("(p t) c -> p t c", t=PACK)
+        out_words = out_1[0].rearrange("p c t -> p (c t)").bitcast(I32)
+        o_bf = sb("o_bf", [P, S, PACK], BF16)
+        o_words = sb("o_words", [P, S], I32)
+        o_scales = sb("o_scales", [P, S], U8)
+        starts = [sum(OUT_CHUNKS[:c]) for c in range(len(OUT_CHUNKS))]
+        at3 = sb("at3", [P, PACK, S], F32)
+        first = sb("first", [P, PACK, S], F32)
+        for t in range(PACK):
+            for start in (0, HALF):
+                fetch((t, start) in N3_ON_SCALAR, at3[:, t, start : start + HALF], h_sb[t], n3_t, start, HALF)
+        for t in range(PACK):
+            nc.vector.scalar_tensor_tensor(first[:, t, :], h_ps[t][:], 0.75, at3[:, t, :], ALU.mult, ALU.mult)
+        for c, width in enumerate(OUT_CHUNKS):
+            start = starts[c]
+            cols = slice(start, start + width)
+            at4 = sb(f"at4_{c}", [P, PACK, width], F32)
+            at5 = sb(f"at5_{c}", [P, PACK, width], F32)
+            second = sb(f"second{c}", [P, PACK, width], F32)
+            result = sb(f"result{c}", [P, PACK, width], F32)
+            for t in range(PACK):
+                fetch(True, at4[:, t, :], h_sb[t], n4_t, start, width)
+                fetch(True, at5[:, t, :], h_sb[t], n5_t, start, width)
+            nc.vector.scalar_tensor_tensor(second[:], at4[:], 0.75, at5[:], ALU.mult, ALU.mult)
+            nc.vector.tensor_tensor(result[:], first[:, :, cols], second[:], ALU.add)
+            nc.sync.dma_start(out_rows[:, :, cols], result[:])
+            nc.vector.tensor_copy(woven(o_bf[:, cols, :]), planar(result[:]))
+            quantise(o_words, o_scales, o_bf, cols)
+            nc.sync.dma_start(out_words[:, cols], o_words[:, cols])
+        for q in range(4):
+            queue = nc.scalar if q % 2 == 0 else nc.sync
+            queue.dma_start(out_2[0, 4 * q : 4 * q + 4, :].bitcast(I32), o_scales[32 * q : 32 * q + 4, :].bitcast(I32))

@@ -19,9 +19,10 @@ P = 128
 PACK = 4
 HALF = S // 2
 QUARTER = S // 4
-OUT_CHUNKS = (128, 128, 128, 128)
-N2_ON_VECTOR = (1, 1)
-N3_ON_SCALAR = ((0, 0),)
+OUT_CHUNKS = (128, 128, 128, 64, 64)
+N1_ON_SCALAR = ((3,256),)
+N2_ON_VECTOR = (1,1,1,1)
+N3_ON_SCALAR = ()
 
 
 def tile_picked_hjoinharmnormdot_none_po_kernel(
@@ -49,16 +50,16 @@ def tile_picked_hjoinharmnormdot_none_po_kernel(
         def load_words(tile, src):
             nc.sync.dma_start(tile[:], src[0].rearrange("p n t -> p (n t)").bitcast(I32))
 
-        def load_scale_rows(tile, src, first):
+        def load_scale_rows(queue, tile, src, first):
             for q in range(4):
-                nc.sync.dma_start(
+                queue.dma_start(
                     tile[32 * q + first : 32 * q + first + 4, :].bitcast(I32),
                     src[0, 4 * q : 4 * q + 4, :].bitcast(I32),
                 )
 
-        def deal(name, raw, dtype, view):
+        def deal(engine, name, raw, dtype, view):
             tile = sb(name, [P, H], dtype)
-            nc.vector.tensor_copy(
+            engine.tensor_copy(
                 tile[:].bitcast(view).rearrange("p (t m) -> p m t", t=PACK),
                 raw[:].bitcast(view).rearrange("p (m t) -> p m t", t=PACK),
             )
@@ -89,6 +90,9 @@ def tile_picked_hjoinharmnormdot_none_po_kernel(
         nc.gpsimd.memset(quarter[:], 0.25)
         nc.gpsimd.memset(half[:], 0.5)
 
+        warm = sb("warm", [P, 1], F32)
+        nc.scalar.activation(warm[:], half[:], ACT.Abs_reciprocal_sqrt)
+
         xw_table = sb("xw_table", [P, T], I32)
         wa_raw = sb("wa_raw", [P, H], I32)
         wb_raw = sb("wb_raw", [P, H], I32)
@@ -97,24 +101,18 @@ def tile_picked_hjoinharmnormdot_none_po_kernel(
         offs_t = load_list("offs_t", offs)
         load_words(xw_table, x_words)
         load_words(wa_raw, w1_words)
-        load_scale_rows(xs_rows, x_scales, 0)
-        load_scale_rows(ws_raw, w1_scales, 0)
-        n1_t = load_list("n1_t", n1)
-        nc.sync.dma_start(xs_runs[0:P:8, :].bitcast(I32), x_scales[0].bitcast(I32))
+        load_scale_rows(nc.sync, xs_rows, x_scales, 0)
+        load_scale_rows(nc.sync, ws_raw, w1_scales, 0)
         hz_t = load_list("hz_t", hz)
+        n1_t = load_list("n1_t", n1)
+        nc.gpsimd.dma_start(xs_runs[0:P:8, :].bitcast(I32), x_scales[0].bitcast(I32))
         load_words(wb_raw, w2_words)
-        load_scale_rows(ws2_raw, w2_scales, 0)
-        nc.sync.dma_start(gn_t[:], gn.rearrange("(p t) o -> p (t o)", t=PACK))
-        nc.sync.dma_start(gm_t[:], gm.rearrange("(p t) o -> p (t o)", t=PACK))
-        n2_t = load_list("n2_t", n2)
-        n3_t = load_list("n3_t", n3)
-        n4_t = load_list("n4_t", n4)
-        n5_t = load_list("n5_t", n5)
+        load_scale_rows(nc.gpsimd, ws2_raw, w2_scales, 0)
 
         xs_offs = sb("xs_offs", [P, S], U8)
         nc.vector.tensor_copy(xs_offs[:], xs_rows[:].indirect(offs_t[:]))
-        w1_t = deal("w1_t", wa_raw, I32, U32)
-        ws1 = deal("ws1", ws_raw, U8, U8)
+        w1_t = deal(nc.vector, "w1_t", wa_raw, I32, U32)
+        ws1 = deal(nc.vector, "ws1", ws_raw, U8, U8)
 
         xw_offs = sb("xw_offs", [P, S], I32)
         nc.vector.tensor_copy(xw_offs[:].bitcast(U32), xw_table[:].bitcast(U32).indirect(offs_t[:]))
@@ -129,6 +127,9 @@ def tile_picked_hjoinharmnormdot_none_po_kernel(
         picked_hz = sb("picked_hz", [P, S], U8)
         nc.vector.tensor_copy(picked_hz[:], xs_runs[:].indirect(hz_t[:]))
         place_scale_rows(xs_hz, picked_hz)
+        nc.sync.dma_start(gn_t[:], gn.rearrange("(p t) o -> p (t o)", t=PACK))
+        nc.sync.dma_start(gm_t[:], gm.rearrange("(p t) o -> p (t o)", t=PACK))
+        n2_t = load_list("n2_t", n2)
         xw_hz = sb("xw_hz", [P, S], I32)
         nc.vector.tensor_copy(xw_hz[:].bitcast(U32), xw_table[:].bitcast(U32).indirect(hz_t[:]))
         def columns(j):
@@ -169,12 +170,15 @@ def tile_picked_hjoinharmnormdot_none_po_kernel(
         for t in range(PACK):
             nc.scalar.activation(y_sb[t][:], y_ps[t][:], ACT.Copy)
 
-        w2_t = deal("w2_t", wb_raw, I32, U32)
-        ws2 = deal("ws2", ws2_raw, U8, U8)
+        w2_t = deal(nc.vector, "w2_t", wb_raw, I32, U32)
+        ws2 = deal(nc.gpsimd, "ws2", ws2_raw, U8, U8)
         load_words(wa_raw, w3_words)
         load_words(wb_raw, w4_words)
-        load_scale_rows(ws_raw, w3_scales, 4)
-        load_scale_rows(ws_raw, w4_scales, 8)
+        load_scale_rows(nc.sync, ws_raw, w3_scales, 4)
+        load_scale_rows(nc.sync, ws_raw, w4_scales, 8)
+        n3_t = load_list("n3_t", n3)
+        n4_t = load_list("n4_t", n4)
+        n5_t = load_list("n5_t", n5)
         d_ps = [psum.tile([P, PACK, QUARTER], F32, name=f"d_ps{j}", tag=f"cols{j}") for j in range(4)]
         for j in range(4):
             for t in range(PACK):
@@ -186,8 +190,14 @@ def tile_picked_hjoinharmnormdot_none_po_kernel(
 
         for t in range(PACK):
             nc.scalar.activation(y_sq[:, t, :], y_ps[t][:], ACT.Square)
+        for t in range(PACK):
             for start in (0, HALF):
-                fetch(False, pa[:, t, start : start + HALF], y_sb[t], n1_t, start, HALF)
+                fetch((t, start) in N1_ON_SCALAR, pa[:, t, start : start + HALF], y_sb[t], n1_t, start, HALF)
+        for t in range(PACK):
+            nc.scalar.activation(pa_sq[:, t, :], pa[:, t, :], ACT.Square)
+            nc.vector.tensor_tensor(squares[:, t, :], y_sq[:, t, :], pa_sq[:, t, :], ALU.add)
+        for t in range(PACK):
+            nc.vector.scalar_tensor_tensor(numer[:, t, :], y_ps[t][:], gn_t[:, t : t + 1], pa[:, t, :], ALU.mult, ALU.mult)
         for j in range(4):
             nc.scalar.activation(d_abs[j][:], d_ps[j][:].rearrange("p t c -> p (t c)"), ACT.Abs)
         for j in range(4):
@@ -196,49 +206,41 @@ def tile_picked_hjoinharmnormdot_none_po_kernel(
                 ACT.Abs_reciprocal_sqrt, bias=half[:], scale=1.0,
             )
         for t in range(PACK):
-            nc.vector.scalar_tensor_tensor(numer[:, t, :], y_ps[t][:], gn_t[:, t : t + 1], pa[:, t, :], ALU.mult, ALU.mult)
-        for t in range(PACK):
             nc.vector.scalar_tensor_tensor(
                 gain_over[t][:].rearrange("p (j c) -> p j c", j=4), d_root[:, :, t, :], gm_t[:, t : t + 1],
                 d_root[:, :, t, :], ALU.mult, ALU.mult,
             )
-        for t in range(PACK):
-            nc.scalar.activation(pa_sq[:, t, :], pa[:, t, :], ACT.Square)
-            nc.vector.tensor_tensor(squares[:, t, :], y_sq[:, t, :], pa_sq[:, t, :], ALU.add)
-        w3_t = deal("w3_t", wa_raw, I32, U32)
-        w4_t = deal("w4_t", wb_raw, I32, U32)
-        ws34 = deal("ws34", ws_raw, U8, U8)
-
-        for start in (0, HALF):
-            for t in range(PACK):
-                fetch(t >= N2_ON_VECTOR[start // HALF], looked[:, t, start : start + HALF], gain_over[t], n2_t, start, HALF)
-            for j in (start // QUARTER, start // QUARTER + 1):
-                nc.vector.tensor_tensor(
-                    woven(z2_bf[:, columns(j), :]), planar(d_ps[j][:]), planar(looked[:, :, columns(j)]), ALU.mult
-                )
-            quantise(z2_words, z2_scales, z2_bf, slice(start, start + HALF))
-
-        h_ps = [psum.tile([P, S], F32, name=f"h_ps{t}", tag=f"rows{t}") for t in range(PACK)]
-        for t in range(PACK):
-            m = slice(P * t, P * (t + 1))
-            nc.tensor.matmul_mx(
-                out=h_ps[t][:], lhsT=w4_t[:, m].bitcast(FP8X4), lhsT_scale=ws34[8:P, m],
-                rhs=z2_words[:].bitcast(FP8X4), rhs_scale=z2_scales[:], start=True, stop=False,
-            )
-
+        w3_t = deal(nc.vector, "w3_t", wa_raw, I32, U32)
+        w4_t = deal(nc.vector, "w4_t", wb_raw, I32, U32)
+        ws34 = deal(nc.vector, "ws34", ws_raw, U8, U8)
         for j in range(4):
             cols = columns(j)
             nc.scalar.activation(root[:, :, cols], squares[:, :, cols], ACT.Abs_reciprocal_sqrt, bias=quarter[:], scale=0.5)
             nc.scalar.activation(inverse[:, :, cols], root[:, :, cols], ACT.Square)
             nc.vector.tensor_tensor(woven(z_bf[:, cols, :]), planar(numer[:, :, cols]), planar(inverse[:, :, cols]), ALU.mult)
             quantise(z_words, z_scales, z_bf, cols)
-
+        for j in range(4):
+            for t in range(PACK):
+                fetch(t >= N2_ON_VECTOR[j], looked[:, t, columns(j)], gain_over[t], n2_t, QUARTER * j, QUARTER)
+            nc.vector.tensor_tensor(
+                woven(z2_bf[:, columns(j), :]), planar(d_ps[j][:]), planar(looked[:, :, columns(j)]), ALU.mult
+            )
+            quantise(z2_words, z2_scales, z2_bf, columns(j))
+        h_ps = [psum.tile([P, S], F32, name=f"h_ps{t}", tag=f"rows{t}") for t in range(PACK)]
         for t in range(PACK):
             m = slice(P * t, P * (t + 1))
             nc.tensor.matmul_mx(
                 out=h_ps[t][:], lhsT=w3_t[:, m].bitcast(FP8X4), lhsT_scale=ws34[4:P, m],
-                rhs=z_words[:].bitcast(FP8X4), rhs_scale=z_scales[:], start=False, stop=True,
+                rhs=z_words[:].bitcast(FP8X4), rhs_scale=z_scales[:], start=True, stop=False,
             )
+        for j in range(4):
+            for t in range(PACK):
+                m = slice(P * t, P * (t + 1))
+                nc.tensor.matmul_mx(
+                    out=h_ps[t][:, columns(j)], lhsT=w4_t[:, m].bitcast(FP8X4), lhsT_scale=ws34[8:P, m],
+                    rhs=z2_words[:, columns(j)].bitcast(FP8X4), rhs_scale=z2_scales[:, columns(j)],
+                    start=False, stop=(j == 3),
+                )
 
         h_sb = [sb(f"h_sb{t}", [P, S], F32) for t in range(PACK)]
         for t in range(PACK):

@@ -19,10 +19,10 @@ P = 128
 PACK = 4
 HALF = S // 2
 QUARTER = S // 4
-OUT_CHUNKS = (128, 128, 128, 64, 64)
-N1_ON_SCALAR = ((3,256),)
+OUT_CHUNKS = (256, 128, 128)
+N1_ON_SCALAR = ()
 N2_ON_VECTOR = (1,1,1,1)
-N3_ON_SCALAR = ()
+N3_ON_SCALAR = 1
 
 
 def tile_picked_hjoinharmnormdot_none_po_kernel(
@@ -36,8 +36,8 @@ def tile_picked_hjoinharmnormdot_none_po_kernel(
         keep = ctx.enter_context(tc.tile_pool(name="keep", bufs=1))
         psum = ctx.enter_context(tc.psum_pool(name="psum", bufs=1))
 
-        def sb(name, shape, dtype):
-            return keep.tile(shape, dtype, name=name, align_bytes=64)
+        def sb(name, shape, dtype, tag=None):
+            return keep.tile(shape, dtype, name=name, tag=tag or name, align_bytes=64)
 
         def load_list(name, src):
             tile = keep.tile([P, S // 16], U16, name=name)
@@ -75,23 +75,20 @@ def tile_picked_hjoinharmnormdot_none_po_kernel(
         def planar(ap):
             return ap.rearrange("p t (c i) -> p c t i", i=4)
 
-        xs_rows = sb("xs_rows", [P, T], U8)
-        xs_runs = sb("xs_runs", [P, T], U8)
+        xs_table = sb("xs_table", [P, T], U8)
         ws_raw = sb("ws_raw", [P, H], U8)
         ws2_raw = sb("ws2_raw", [P, H], U8)
+        xs_offs = sb("xs_offs", [P, S], U8)
         xs_hz = sb("xs_hz", [P, S], U8)
-        nc.gpsimd.memset(ws_raw[:].bitcast(I32), 0)
-        nc.vector.memset(xs_rows[:, : T // 2].bitcast(I32), 0)
-        nc.gpsimd.memset(xs_rows[:, T // 2 :].bitcast(I32), 0)
-        for tile in (xs_runs, ws2_raw, xs_hz):
-            nc.gpsimd.memset(tile[:].bitcast(I32), 0)
         quarter = sb("quarter", [P, 1], F32)
         half = sb("half", [P, 1], F32)
-        nc.gpsimd.memset(quarter[:], 0.25)
-        nc.gpsimd.memset(half[:], 0.5)
-
-        warm = sb("warm", [P, 1], F32)
-        nc.scalar.activation(warm[:], half[:], ACT.Abs_reciprocal_sqrt)
+        nc.gpsimd.memset(ws_raw[:].bitcast(I32), 0)
+        nc.gpsimd.memset(xs_table[:].bitcast(I32), 0)
+        nc.gpsimd.memset(ws2_raw[:].bitcast(I32), 0)
+        for tile in (xs_offs, xs_hz):
+            nc.vector.memset(tile[:].bitcast(I32), 0)
+        nc.vector.memset(quarter[:], 0.25)
+        nc.vector.memset(half[:], 0.5)
 
         xw_table = sb("xw_table", [P, T], I32)
         wa_raw = sb("wa_raw", [P, H], I32)
@@ -99,20 +96,24 @@ def tile_picked_hjoinharmnormdot_none_po_kernel(
         gn_t = sb("gn_t", [P, PACK], F32)
         gm_t = sb("gm_t", [P, PACK], F32)
         offs_t = load_list("offs_t", offs)
+        nc.sync.dma_start(xs_table[0:P:8, :].bitcast(I32), x_scales[0].bitcast(I32))
+        load_scale_rows(nc.scalar, ws_raw, w1_scales, 0)
+        hz_t = load_list("hz_t", hz)
         load_words(xw_table, x_words)
         load_words(wa_raw, w1_words)
-        load_scale_rows(nc.sync, xs_rows, x_scales, 0)
-        load_scale_rows(nc.sync, ws_raw, w1_scales, 0)
-        hz_t = load_list("hz_t", hz)
-        n1_t = load_list("n1_t", n1)
-        nc.gpsimd.dma_start(xs_runs[0:P:8, :].bitcast(I32), x_scales[0].bitcast(I32))
-        load_words(wb_raw, w2_words)
         load_scale_rows(nc.gpsimd, ws2_raw, w2_scales, 0)
 
-        xs_offs = sb("xs_offs", [P, S], U8)
-        nc.vector.tensor_copy(xs_offs[:], xs_rows[:].indirect(offs_t[:]))
-        w1_t = deal(nc.vector, "w1_t", wa_raw, I32, U32)
+        warm = sb("warm", [P, 1], F32)
+        nc.scalar.activation(warm[:], half[:], ACT.Abs_reciprocal_sqrt)
+        picked_offs = sb("picked_offs", [P, S], U8)
+        picked_hz = sb("picked_hz", [P, S], U8)
+        nc.vector.tensor_copy(picked_offs[:], xs_table[:].indirect(offs_t[:]))
+        place_scale_rows(xs_offs, picked_offs)
+        nc.vector.tensor_copy(picked_hz[:], xs_table[:].indirect(hz_t[:]))
         ws1 = deal(nc.vector, "ws1", ws_raw, U8, U8)
+        w1_t = deal(nc.vector, "w1_t", wa_raw, I32, U32)
+        n1_t = load_list("n1_t", n1)
+        load_words(wb_raw, w2_words)
 
         xw_offs = sb("xw_offs", [P, S], I32)
         nc.vector.tensor_copy(xw_offs[:].bitcast(U32), xw_table[:].bitcast(U32).indirect(offs_t[:]))
@@ -124,13 +125,11 @@ def tile_picked_hjoinharmnormdot_none_po_kernel(
                 rhs=xw_offs[:].bitcast(FP8X4), rhs_scale=xs_offs[:], start=True, stop=True,
             )
 
-        picked_hz = sb("picked_hz", [P, S], U8)
-        nc.vector.tensor_copy(picked_hz[:], xs_runs[:].indirect(hz_t[:]))
         place_scale_rows(xs_hz, picked_hz)
         nc.sync.dma_start(gn_t[:], gn.rearrange("(p t) o -> p (t o)", t=PACK))
         nc.sync.dma_start(gm_t[:], gm.rearrange("(p t) o -> p (t o)", t=PACK))
         n2_t = load_list("n2_t", n2)
-        xw_hz = sb("xw_hz", [P, S], I32)
+        xw_hz = sb("xw_hz", [P, S], I32, tag="wa_raw")
         nc.vector.tensor_copy(xw_hz[:].bitcast(U32), xw_table[:].bitcast(U32).indirect(hz_t[:]))
         def columns(j):
             return slice(QUARTER * j, QUARTER * (j + 1))
@@ -172,7 +171,8 @@ def tile_picked_hjoinharmnormdot_none_po_kernel(
 
         w2_t = deal(nc.vector, "w2_t", wb_raw, I32, U32)
         ws2 = deal(nc.gpsimd, "ws2", ws2_raw, U8, U8)
-        load_words(wa_raw, w3_words)
+        wc_raw = sb("wc_raw", [P, N], I32, tag="xw_offs")
+        load_words(wc_raw, w3_words)
         load_words(wb_raw, w4_words)
         load_scale_rows(nc.sync, ws_raw, w3_scales, 4)
         load_scale_rows(nc.sync, ws_raw, w4_scales, 8)
@@ -210,7 +210,7 @@ def tile_picked_hjoinharmnormdot_none_po_kernel(
                 gain_over[t][:].rearrange("p (j c) -> p j c", j=4), d_root[:, :, t, :], gm_t[:, t : t + 1],
                 d_root[:, :, t, :], ALU.mult, ALU.mult,
             )
-        w3_t = deal(nc.vector, "w3_t", wa_raw, I32, U32)
+        w3_t = deal(nc.vector, "w3_t", wc_raw, I32, U32)
         w4_t = deal(nc.vector, "w4_t", wb_raw, I32, U32)
         ws34 = deal(nc.vector, "ws34", ws_raw, U8, U8)
         for j in range(4):
@@ -257,11 +257,15 @@ def tile_picked_hjoinharmnormdot_none_po_kernel(
         starts = [sum(OUT_CHUNKS[:c]) for c in range(len(OUT_CHUNKS))]
         at3 = sb("at3", [P, PACK, S], F32)
         first = sb("first", [P, PACK, S], F32)
+        def first_product(t, start):
+            both = slice(start, start + HALF)
+            fetch(start == HALF and t >= PACK - N3_ON_SCALAR, at3[:, t, both], h_sb[t], n3_t, start, HALF)
+            nc.vector.scalar_tensor_tensor(first[:, t, both], h_ps[t][:, both], 0.75, at3[:, t, both], ALU.mult, ALU.mult)
+
         for t in range(PACK):
-            for start in (0, HALF):
-                fetch((t, start) in N3_ON_SCALAR, at3[:, t, start : start + HALF], h_sb[t], n3_t, start, HALF)
-        for t in range(PACK):
-            nc.vector.scalar_tensor_tensor(first[:, t, :], h_ps[t][:], 0.75, at3[:, t, :], ALU.mult, ALU.mult)
+            first_product(t, 0)
+        for t in range(PACK - N3_ON_SCALAR):
+            first_product(t, HALF)
         for c, width in enumerate(OUT_CHUNKS):
             start = starts[c]
             cols = slice(start, start + width)
@@ -272,6 +276,9 @@ def tile_picked_hjoinharmnormdot_none_po_kernel(
             for t in range(PACK):
                 fetch(True, at4[:, t, :], h_sb[t], n4_t, start, width)
                 fetch(True, at5[:, t, :], h_sb[t], n5_t, start, width)
+            if c == 1:
+                for t in range(PACK - N3_ON_SCALAR, PACK):
+                    first_product(t, HALF)
             nc.vector.scalar_tensor_tensor(second[:], at4[:], 0.75, at5[:], ALU.mult, ALU.mult)
             nc.vector.tensor_tensor(result[:], first[:, :, cols], second[:], ALU.add)
             nc.sync.dma_start(out_rows[:, :, cols], result[:])

@@ -22,7 +22,7 @@ QUARTER = S // 4
 OUT_CHUNKS = (256, 128, 128)
 N1_ON_SCALAR = ()
 N2_ON_VECTOR = (1,1,1,1)
-N3_ON_SCALAR = 1
+N3_ON_VECTOR = ((1, 0),)
 
 
 def tile_picked_hjoinharmnormdot_none_po_kernel(
@@ -82,13 +82,13 @@ def tile_picked_hjoinharmnormdot_none_po_kernel(
         xs_hz = sb("xs_hz", [P, S], U8)
         quarter = sb("quarter", [P, 1], F32)
         half = sb("half", [P, 1], F32)
-        nc.gpsimd.memset(ws_raw[:].bitcast(I32), 0)
         nc.gpsimd.memset(xs_table[:].bitcast(I32), 0)
+        nc.gpsimd.memset(ws_raw[:].bitcast(I32), 0)
         nc.gpsimd.memset(ws2_raw[:].bitcast(I32), 0)
+        nc.gpsimd.memset(half[:], 0.5)
         for tile in (xs_offs, xs_hz):
             nc.vector.memset(tile[:].bitcast(I32), 0)
         nc.vector.memset(quarter[:], 0.25)
-        nc.vector.memset(half[:], 0.5)
 
         xw_table = sb("xw_table", [P, T], I32)
         wa_raw = sb("wa_raw", [P, H], I32)
@@ -259,28 +259,27 @@ def tile_picked_hjoinharmnormdot_none_po_kernel(
         first = sb("first", [P, PACK, S], F32)
         def first_product(t, start):
             both = slice(start, start + HALF)
-            fetch(start == HALF and t >= PACK - N3_ON_SCALAR, at3[:, t, both], h_sb[t], n3_t, start, HALF)
+            fetch((t, start) not in N3_ON_VECTOR, at3[:, t, both], h_sb[t], n3_t, start, HALF)
             nc.vector.scalar_tensor_tensor(first[:, t, both], h_ps[t][:, both], 0.75, at3[:, t, both], ALU.mult, ALU.mult)
 
-        for t in range(PACK):
-            first_product(t, 0)
-        for t in range(PACK - N3_ON_SCALAR):
-            first_product(t, HALF)
+        for t, start in N3_ON_VECTOR:
+            first_product(t, start)
         for c, width in enumerate(OUT_CHUNKS):
             start = starts[c]
             cols = slice(start, start + width)
             at4 = sb(f"at4_{c}", [P, PACK, width], F32)
-            at5 = sb(f"at5_{c}", [P, PACK, width], F32)
             second = sb(f"second{c}", [P, PACK, width], F32)
             result = sb(f"result{c}", [P, PACK, width], F32)
             for t in range(PACK):
                 fetch(True, at4[:, t, :], h_sb[t], n4_t, start, width)
-                fetch(True, at5[:, t, :], h_sb[t], n5_t, start, width)
-            if c == 1:
-                for t in range(PACK - N3_ON_SCALAR, PACK):
-                    first_product(t, HALF)
-            nc.vector.scalar_tensor_tensor(second[:], at4[:], 0.75, at5[:], ALU.mult, ALU.mult)
-            nc.vector.tensor_tensor(result[:], first[:, :, cols], second[:], ALU.add)
+                nc.vector.tensor_tensor(
+                    second[:, t, :], h_sb[t][:].indirect(entries(n5_t, start, width)), at4[:, t, :], ALU.mult
+                )
+            if start % HALF == 0:
+                for t in range(PACK):
+                    if (t, start) not in N3_ON_VECTOR:
+                        first_product(t, start)
+            nc.vector.scalar_tensor_tensor(result[:], second[:], 0.75, first[:, :, cols], ALU.mult, ALU.add)
             nc.sync.dma_start(out_rows[:, :, cols], result[:])
             nc.vector.tensor_copy(woven(o_bf[:, cols, :]), planar(result[:]))
             quantise(o_words, o_scales, o_bf, cols)

@@ -1,8 +1,9 @@
 from contextlib import ExitStack
 
 import concourse.mybir as mybir
+from concourse.masks import make_identity
 
-K, T, S, N, H = 512, 2048, 512, 512, 512
+T, S, H, N = 2048, 512, 512, 512
 FLOPS = 4 * 2 * 512 * 512 * 512
 
 F32 = mybir.dt.float32
@@ -16,13 +17,17 @@ ACT = mybir.ActivationFunctionType
 ALU = mybir.AluOpType
 
 P = 128
-PACK = 4
+PLANES = 4
+QUADRANTS = 4
+QUARTERS = 4
+QUARTER = S // QUARTERS
 HALF = S // 2
-QUARTER = S // 4
-OUT_CHUNKS = (256, 128, 128)
-N1_ON_SCALAR = ()
-N2_ON_VECTOR = (1,1,1,1)
-N3_ON_VECTOR = ((1, 0),)
+W3_BASE, W4_BASE = 4, 8
+
+OUT_CHUNKS = (HALF, QUARTER, QUARTER)
+N3_PLANE_ON_VECTOR = 1
+N5_PLANES_ON_SCALAR = 2
+CHUNK_WOVEN_ON_SCALAR = 1
 
 
 def tile_picked_hjoinharmnormdot_none_po_kernel(
@@ -44,120 +49,30 @@ def tile_picked_hjoinharmnormdot_none_po_kernel(
             nc.sync.dma_start(tile[:], src)
             return tile
 
-        def entries(lst, start, count):
-            return lst[:, start // 16 : (start + count) // 16]
-
         def load_words(tile, src):
             nc.sync.dma_start(tile[:], src[0].rearrange("p n t -> p (n t)").bitcast(I32))
 
-        def load_scale_rows(queue, tile, src, first):
-            for q in range(4):
+        def load_scale_rows(queue, tile, src, base):
+            for q in range(QUADRANTS):
                 queue.dma_start(
-                    tile[32 * q + first : 32 * q + first + 4, :].bitcast(I32),
+                    tile[32 * q + base : 32 * q + base + 4, :].bitcast(I32),
                     src[0, 4 * q : 4 * q + 4, :].bitcast(I32),
                 )
-
-        def deal(engine, name, raw, dtype, view):
-            tile = sb(name, [P, H], dtype)
-            engine.tensor_copy(
-                tile[:].bitcast(view).rearrange("p (t m) -> p m t", t=PACK),
-                raw[:].bitcast(view).rearrange("p (m t) -> p m t", t=PACK),
-            )
-            return tile
 
         def place_scale_rows(dst, picked):
             for r in range(4):
                 nc.sync.dma_start(dst[r:P:32, :].bitcast(I32), picked[8 * r : P : 32, :].bitcast(I32))
 
-        def woven(ap):
-            return ap.rearrange("p (c i) t -> p c t i", i=4)
-
-        def planar(ap):
-            return ap.rearrange("p t (c i) -> p c t i", i=4)
-
-        xs_table = sb("xs_table", [P, T], U8)
-        ws_raw = sb("ws_raw", [P, H], U8)
-        ws2_raw = sb("ws2_raw", [P, H], U8)
-        xs_offs = sb("xs_offs", [P, S], U8)
-        xs_hz = sb("xs_hz", [P, S], U8)
-        quarter = sb("quarter", [P, 1], F32)
-        half = sb("half", [P, 1], F32)
-        nc.gpsimd.memset(xs_table[:].bitcast(I32), 0)
-        nc.gpsimd.memset(ws_raw[:].bitcast(I32), 0)
-        nc.gpsimd.memset(ws2_raw[:].bitcast(I32), 0)
-        nc.gpsimd.memset(half[:], 0.5)
-        for tile in (xs_offs, xs_hz):
-            nc.vector.memset(tile[:].bitcast(I32), 0)
-        nc.vector.memset(quarter[:], 0.25)
-
-        xw_table = sb("xw_table", [P, T], I32)
-        wa_raw = sb("wa_raw", [P, H], I32)
-        wb_raw = sb("wb_raw", [P, H], I32)
-        gn_t = sb("gn_t", [P, PACK], F32)
-        gm_t = sb("gm_t", [P, PACK], F32)
-        offs_t = load_list("offs_t", offs)
-        nc.sync.dma_start(xs_table[0:P:8, :].bitcast(I32), x_scales[0].bitcast(I32))
-        load_scale_rows(nc.scalar, ws_raw, w1_scales, 0)
-        hz_t = load_list("hz_t", hz)
-        load_words(xw_table, x_words)
-        load_words(wa_raw, w1_words)
-        load_scale_rows(nc.gpsimd, ws2_raw, w2_scales, 0)
-
-        warm = sb("warm", [P, 1], F32)
-        nc.scalar.activation(warm[:], half[:], ACT.Abs_reciprocal_sqrt)
-        picked_offs = sb("picked_offs", [P, S], U8)
-        picked_hz = sb("picked_hz", [P, S], U8)
-        nc.vector.tensor_copy(picked_offs[:], xs_table[:].indirect(offs_t[:]))
-        place_scale_rows(xs_offs, picked_offs)
-        nc.vector.tensor_copy(picked_hz[:], xs_table[:].indirect(hz_t[:]))
-        ws1 = deal(nc.vector, "ws1", ws_raw, U8, U8)
-        w1_t = deal(nc.vector, "w1_t", wa_raw, I32, U32)
-        n1_t = load_list("n1_t", n1)
-        load_words(wb_raw, w2_words)
-
-        xw_offs = sb("xw_offs", [P, S], I32)
-        nc.vector.tensor_copy(xw_offs[:].bitcast(U32), xw_table[:].bitcast(U32).indirect(offs_t[:]))
-        y_ps = [psum.tile([P, S], F32, name=f"y_ps{t}", tag=f"rows{t}") for t in range(PACK)]
-        for t in range(PACK):
-            m = slice(P * t, P * (t + 1))
-            nc.tensor.matmul_mx(
-                out=y_ps[t][:], lhsT=w1_t[:, m].bitcast(FP8X4), lhsT_scale=ws1[:, m],
-                rhs=xw_offs[:].bitcast(FP8X4), rhs_scale=xs_offs[:], start=True, stop=True,
+        def deal(engine, name, raw, dtype, view):
+            tile = sb(name, [P, H], dtype)
+            engine.tensor_copy(
+                tile[:].bitcast(view).rearrange("p (t m) -> p m t", t=PLANES),
+                raw[:].bitcast(view).rearrange("p (m t) -> p m t", t=PLANES),
             )
+            return tile
 
-        place_scale_rows(xs_hz, picked_hz)
-        nc.sync.dma_start(gn_t[:], gn.rearrange("(p t) o -> p (t o)", t=PACK))
-        nc.sync.dma_start(gm_t[:], gm.rearrange("(p t) o -> p (t o)", t=PACK))
-        n2_t = load_list("n2_t", n2)
-        xw_hz = sb("xw_hz", [P, S], I32, tag="wa_raw")
-        nc.vector.tensor_copy(xw_hz[:].bitcast(U32), xw_table[:].bitcast(U32).indirect(hz_t[:]))
-        def columns(j):
-            return slice(QUARTER * j, QUARTER * (j + 1))
-
-        y_sb = [sb(f"y_sb{t}", [P, S], F32) for t in range(PACK)]
-        y_sq = sb("y_sq", [P, PACK, S], F32)
-        pa = sb("pa", [P, PACK, S], F32)
-        pa_sq = sb("pa_sq", [P, PACK, S], F32)
-        squares = sb("squares", [P, PACK, S], F32)
-        root = sb("root", [P, PACK, S], F32)
-        numer = sb("numer", [P, PACK, S], F32)
-        inverse = sb("inverse", [P, PACK, S], F32)
-        z_bf = sb("z_bf", [P, S, PACK], BF16)
-        z_words = sb("z_words", [P, S], U32)
-        z_scales = sb("z_scales", [P, S], U8)
-        d_abs = [sb(f"d_abs{j}", [P, S], F32) for j in range(4)]
-        d_root = sb("d_root", [P, 4, PACK, QUARTER], F32)
-        gain_over = [sb(f"gain_over{t}", [P, S], F32) for t in range(PACK)]
-        looked = sb("looked", [P, PACK, S], F32)
-        z2_bf = sb("z2_bf", [P, S, PACK], BF16)
-        z2_words = sb("z2_words", [P, S], U32)
-        z2_scales = sb("z2_scales", [P, S], U8)
-
-        def quantise(words, scales, values, cols):
-            nc.vector.quantize_mx(
-                out=words[:, cols].bitcast(FP8X4), scales=scales[:, cols],
-                in_=values[:, cols, :].rearrange("p c t -> p (c t)"),
-            )
+        def entries(lst, start, count):
+            return lst[:, start // 16 : (start + count) // 16]
 
         def fetch(on_scalar, dst, window, lst, start, count):
             picked = window[:].indirect(entries(lst, start, count))
@@ -166,124 +81,259 @@ def tile_picked_hjoinharmnormdot_none_po_kernel(
             else:
                 nc.vector.tensor_copy(dst, picked)
 
-        for t in range(PACK):
+        def woven(ap):
+            return ap.rearrange("p (c i) t -> p c t i", i=4)
+
+        def planar(ap):
+            return ap.rearrange("p t (c i) -> p c t i", i=4)
+
+        def quantise(words, scales, values, cols):
+            nc.vector.quantize_mx(
+                out=words[:, cols].bitcast(FP8X4), scales=scales[:, cols],
+                in_=values[:, cols, :].rearrange("p c t -> p (c t)"),
+            )
+
+        def product(out, words, scales, base, t, moving_words, moving_scales, cols, start, stop):
+            m = slice(P * t, P * (t + 1))
+            nc.tensor.matmul_mx(
+                out=out, lhsT=words[:, m].bitcast(FP8X4), lhsT_scale=scales[base:P, m],
+                rhs=moving_words[:, cols].bitcast(FP8X4), rhs_scale=moving_scales[:, cols],
+                start=start, stop=stop,
+            )
+
+        def quarter_columns(j):
+            return slice(QUARTER * j, QUARTER * (j + 1))
+
+        all_columns = slice(0, S)
+
+        xs_table = sb("xs_table", [P, T], U8)
+        ws134_raw = sb("ws134_raw", [P, H], U8)
+        ws2_raw = sb("ws2_raw", [P, H], U8)
+        xs_offs = sb("xs_offs", [P, S], U8)
+        xs_hz = sb("xs_hz", [P, S], U8)
+        one_quarter = sb("one_quarter", [P, 1], F32)
+        one_half = sb("one_half", [P, 1], F32)
+        nc.gpsimd.memset(xs_table[:].bitcast(I32), 0)
+        nc.gpsimd.memset(ws134_raw[:].bitcast(I32), 0)
+        nc.gpsimd.memset(ws2_raw[:].bitcast(I32), 0)
+        nc.gpsimd.memset(one_half[:], 0.5)
+        for tile in (xs_offs, xs_hz):
+            nc.vector.memset(tile[:].bitcast(I32), 0)
+        nc.vector.memset(one_quarter[:], 0.25)
+
+        xw_table = sb("xw_table", [P, T], I32)
+        w1_raw = sb("w1_raw", [P, H], I32)
+        w24_raw = sb("w24_raw", [P, H], I32)
+        gn_t = sb("gn_t", [P, PLANES], F32)
+        gm_t = sb("gm_t", [P, PLANES], F32)
+        offs_t = load_list("offs_t", offs)
+        nc.sync.dma_start(xs_table[0:P:8, :].bitcast(I32), x_scales[0].bitcast(I32))
+        load_scale_rows(nc.scalar, ws134_raw, w1_scales, 0)
+        hz_t = load_list("hz_t", hz)
+        load_words(xw_table, x_words)
+        load_words(w1_raw, w1_words)
+        load_scale_rows(nc.gpsimd, ws2_raw, w2_scales, 0)
+
+        warm = sb("warm", [P, 1], F32)
+        nc.scalar.activation(warm[:], one_half[:], ACT.Abs_reciprocal_sqrt)
+
+        picked_offs = sb("picked_offs", [P, S], U8)
+        picked_hz = sb("picked_hz", [P, S], U8)
+        nc.vector.tensor_copy(picked_offs[:], xs_table[:].indirect(offs_t[:]))
+        place_scale_rows(xs_offs, picked_offs)
+        nc.vector.tensor_copy(picked_hz[:], xs_table[:].indirect(hz_t[:]))
+        ws1 = deal(nc.vector, "ws1", ws134_raw, U8, U8)
+        w1_t = deal(nc.vector, "w1_t", w1_raw, I32, U32)
+        n1_t = load_list("n1_t", n1)
+        load_words(w24_raw, w2_words)
+
+        xw_offs = sb("xw_offs", [P, S], I32)
+        nc.vector.tensor_copy(xw_offs[:].bitcast(U32), xw_table[:].bitcast(U32).indirect(offs_t[:]))
+        y_ps = [psum.tile([P, S], F32, name=f"y_ps{t}", tag=f"plane{t}") for t in range(PLANES)]
+        for t in range(PLANES):
+            product(y_ps[t][:], w1_t, ws1, 0, t, xw_offs, xs_offs, all_columns, True, True)
+
+        place_scale_rows(xs_hz, picked_hz)
+        nc.sync.dma_start(gn_t[:], gn.rearrange("(p t) o -> p (t o)", t=PLANES))
+        nc.sync.dma_start(gm_t[:], gm.rearrange("(p t) o -> p (t o)", t=PLANES))
+        n2_t = load_list("n2_t", n2)
+        xw_hz = sb("xw_hz", [P, S], I32, tag="w1_raw")
+        nc.vector.tensor_copy(xw_hz[:].bitcast(U32), xw_table[:].bitcast(U32).indirect(hz_t[:]))
+
+        y_sb = [sb(f"y_sb{t}", [P, S], F32) for t in range(PLANES)]
+        y_sq = sb("y_sq", [P, PLANES, S], F32)
+        pa = sb("pa", [P, PLANES, S], F32)
+        pa_sq = sb("pa_sq", [P, PLANES, S], F32)
+        y_root = [sb(f"y_root{j}", [P, H], F32) for j in range(QUARTERS)]
+        numer = sb("numer", [P, PLANES, S], F32)
+        inverse = [sb(f"inverse{j}", [P, H], F32) for j in range(QUARTERS)]
+        z_bf = sb("z_bf", [P, S, PLANES], BF16)
+        z_words = sb("z_words", [P, S], U32)
+        z_scales = sb("z_scales", [P, S], U8)
+        d_abs = [sb(f"d_abs{j}", [P, PLANES * QUARTER], F32) for j in range(QUARTERS)]
+        d_root = sb("d_root", [P, QUARTERS, PLANES, QUARTER], F32)
+        gain_over = [sb(f"gain_over{t}", [P, S], F32) for t in range(PLANES)]
+        gain_at2 = sb("gain_at2", [P, PLANES, S], F32)
+        z2_bf = sb("z2_bf", [P, S, PLANES], BF16)
+        z2_words = sb("z2_words", [P, S], U32)
+        z2_scales = sb("z2_scales", [P, S], U8)
+
+        for t in range(PLANES):
             nc.scalar.activation(y_sb[t][:], y_ps[t][:], ACT.Copy)
 
-        w2_t = deal(nc.vector, "w2_t", wb_raw, I32, U32)
+        identity = sb("identity", [P, P], F32)
+        make_identity(nc, identity[:])
+
+        w2_t = deal(nc.vector, "w2_t", w24_raw, I32, U32)
         ws2 = deal(nc.gpsimd, "ws2", ws2_raw, U8, U8)
-        wc_raw = sb("wc_raw", [P, N], I32, tag="xw_offs")
-        load_words(wc_raw, w3_words)
-        load_words(wb_raw, w4_words)
-        load_scale_rows(nc.sync, ws_raw, w3_scales, 4)
-        load_scale_rows(nc.sync, ws_raw, w4_scales, 8)
+        w3_raw = sb("w3_raw", [P, N], I32, tag="xw_offs")
+        load_words(w3_raw, w3_words)
+        load_words(w24_raw, w4_words)
+        load_scale_rows(nc.sync, ws134_raw, w3_scales, W3_BASE)
+        load_scale_rows(nc.sync, ws134_raw, w4_scales, W4_BASE)
         n3_t = load_list("n3_t", n3)
         n4_t = load_list("n4_t", n4)
         n5_t = load_list("n5_t", n5)
-        d_ps = [psum.tile([P, PACK, QUARTER], F32, name=f"d_ps{j}", tag=f"cols{j}") for j in range(4)]
-        for j in range(4):
-            for t in range(PACK):
-                m = slice(P * t, P * (t + 1))
-                nc.tensor.matmul_mx(
-                    out=d_ps[j][:, t, :], lhsT=w2_t[:, m].bitcast(FP8X4), lhsT_scale=ws2[:, m],
-                    rhs=xw_hz[:, columns(j)].bitcast(FP8X4), rhs_scale=xs_hz[:, columns(j)], start=True, stop=True,
-                )
 
-        for t in range(PACK):
+        d_ps = [psum.tile([P, PLANES, QUARTER], F32, name=f"d_ps{j}", tag=f"quarter{j}") for j in range(QUARTERS)]
+        for j in range(QUARTERS):
+            for t in range(PLANES):
+                product(d_ps[j][:, t, :], w2_t, ws2, 0, t, xw_hz, xs_hz, quarter_columns(j), True, True)
+
+        for t in range(PLANES):
             nc.scalar.activation(y_sq[:, t, :], y_ps[t][:], ACT.Square)
-        for t in range(PACK):
-            for start in (0, HALF):
-                fetch((t, start) in N1_ON_SCALAR, pa[:, t, start : start + HALF], y_sb[t], n1_t, start, HALF)
-        for t in range(PACK):
-            nc.scalar.activation(pa_sq[:, t, :], pa[:, t, :], ACT.Square)
-            nc.vector.tensor_tensor(squares[:, t, :], y_sq[:, t, :], pa_sq[:, t, :], ALU.add)
-        for t in range(PACK):
-            nc.vector.scalar_tensor_tensor(numer[:, t, :], y_ps[t][:], gn_t[:, t : t + 1], pa[:, t, :], ALU.mult, ALU.mult)
-        for j in range(4):
+        for start in (0, HALF):
+            for t in range(PLANES):
+                fetch(False, pa[:, t, start : start + HALF], y_sb[t], n1_t, start, HALF)
+
+        for j in range(QUARTERS):
             nc.scalar.activation(d_abs[j][:], d_ps[j][:].rearrange("p t c -> p (t c)"), ACT.Abs)
-        for j in range(4):
+        for j in range(QUARTERS):
             nc.scalar.activation(
                 d_root[:, j, :, :].rearrange("p t c -> p (t c)"), d_abs[j][:],
-                ACT.Abs_reciprocal_sqrt, bias=half[:], scale=1.0,
+                ACT.Abs_reciprocal_sqrt, bias=one_half[:], scale=1.0,
             )
-        for t in range(PACK):
+
+        for j in range(QUARTERS):
+            cols = quarter_columns(j)
+            nc.vector.tensor_tensor(pa_sq[:, :, cols], pa[:, :, cols], pa[:, :, cols], ALU.mult)
+        for t in range(PLANES):
             nc.vector.scalar_tensor_tensor(
-                gain_over[t][:].rearrange("p (j c) -> p j c", j=4), d_root[:, :, t, :], gm_t[:, t : t + 1],
-                d_root[:, :, t, :], ALU.mult, ALU.mult,
+                numer[:, t, :], y_sb[t][:], gn_t[:, t : t + 1], pa[:, t, :], ALU.mult, ALU.mult
             )
-        w3_t = deal(nc.vector, "w3_t", wc_raw, I32, U32)
-        w4_t = deal(nc.vector, "w4_t", wb_raw, I32, U32)
-        ws34 = deal(nc.vector, "ws34", ws_raw, U8, U8)
-        for j in range(4):
-            cols = columns(j)
-            nc.scalar.activation(root[:, :, cols], squares[:, :, cols], ACT.Abs_reciprocal_sqrt, bias=quarter[:], scale=0.5)
-            nc.scalar.activation(inverse[:, :, cols], root[:, :, cols], ACT.Square)
-            nc.vector.tensor_tensor(woven(z_bf[:, cols, :]), planar(numer[:, :, cols]), planar(inverse[:, :, cols]), ALU.mult)
-            quantise(z_words, z_scales, z_bf, cols)
-        for j in range(4):
-            for t in range(PACK):
-                fetch(t >= N2_ON_VECTOR[j], looked[:, t, columns(j)], gain_over[t], n2_t, QUARTER * j, QUARTER)
+
+        for t in range(PLANES):
+            nc.vector.scalar_tensor_tensor(
+                gain_over[t][:].rearrange("p (j c) -> p j c", j=QUARTERS), d_root[:, :, t, :],
+                gm_t[:, t : t + 1], d_root[:, :, t, :], ALU.mult, ALU.mult,
+            )
+        w3_t = deal(nc.vector, "w3_t", w3_raw, I32, U32)
+        w4_t = deal(nc.vector, "w4_t", w24_raw, I32, U32)
+        ws34 = deal(nc.vector, "ws34", ws134_raw, U8, U8)
+
+        squares_ps = [psum.tile([P, PLANES, P], F32, name=f"squares_ps{j}", tag=f"plane{j}") for j in range(QUARTERS)]
+        for term, is_first in ((y_sq, True), (pa_sq, False)):
+            for j in range(QUARTERS):
+                for t in range(PLANES):
+                    nc.tensor.matmul(
+                        squares_ps[j][:, t, :], lhsT=term[:, t, quarter_columns(j)], rhs=identity[:],
+                        start=is_first and t == 0, stop=not is_first and t == PLANES - 1, is_transpose=True,
+                    )
+
+        for j in range(QUARTERS):
+            cols = quarter_columns(j)
+            nc.scalar.activation(
+                y_root[j][:], squares_ps[j][:].rearrange("c t p -> c (t p)"),
+                ACT.Abs_reciprocal_sqrt, bias=one_quarter[:], scale=0.5,
+            )
+            nc.scalar.activation(inverse[j][:], y_root[j][:], ACT.Square)
+            inverse_ps = psum.tile([P, PLANES, QUARTER], F32, name=f"inverse_ps{j}", tag=f"plane{j}")
+            for t in range(PLANES):
+                nc.tensor.transpose(inverse_ps[:, t, :], inverse[j][:, P * t : P * (t + 1)], identity[:])
             nc.vector.tensor_tensor(
-                woven(z2_bf[:, columns(j), :]), planar(d_ps[j][:]), planar(looked[:, :, columns(j)]), ALU.mult
+                woven(z_bf[:, cols, :]), planar(inverse_ps[:]), planar(numer[:, :, cols]), ALU.mult
             )
-            quantise(z2_words, z2_scales, z2_bf, columns(j))
-        h_ps = [psum.tile([P, S], F32, name=f"h_ps{t}", tag=f"rows{t}") for t in range(PACK)]
-        for t in range(PACK):
-            m = slice(P * t, P * (t + 1))
-            nc.tensor.matmul_mx(
-                out=h_ps[t][:], lhsT=w3_t[:, m].bitcast(FP8X4), lhsT_scale=ws34[4:P, m],
-                rhs=z_words[:].bitcast(FP8X4), rhs_scale=z_scales[:], start=True, stop=False,
+            quantise(z_words, z_scales, z_bf, cols)
+
+        for j in range(QUARTERS):
+            cols = quarter_columns(j)
+            for t in range(PLANES):
+                fetch(True, gain_at2[:, t, cols], gain_over[t], n2_t, cols.start, QUARTER)
+            nc.vector.tensor_tensor(
+                woven(z2_bf[:, cols, :]), planar(d_ps[j][:]), planar(gain_at2[:, :, cols]), ALU.mult
             )
-        for j in range(4):
-            for t in range(PACK):
-                m = slice(P * t, P * (t + 1))
-                nc.tensor.matmul_mx(
-                    out=h_ps[t][:, columns(j)], lhsT=w4_t[:, m].bitcast(FP8X4), lhsT_scale=ws34[8:P, m],
-                    rhs=z2_words[:, columns(j)].bitcast(FP8X4), rhs_scale=z2_scales[:, columns(j)],
-                    start=False, stop=(j == 3),
+            quantise(z2_words, z2_scales, z2_bf, cols)
+
+        h_ps = {}
+        for start, banks in ((0, "plane"), (HALF, "quarter")):
+            for t in range(PLANES):
+                h_ps[t, start] = psum.tile([P, HALF], F32, name=f"h_ps{t}_{start}", tag=f"{banks}{t}")
+                product(
+                    h_ps[t, start][:], w3_t, ws34, W3_BASE, t, z_words, z_scales,
+                    slice(start, start + HALF), True, False,
                 )
+            for offset in (0, QUARTER):
+                cols = slice(start + offset, start + offset + QUARTER)
+                for t in range(PLANES):
+                    product(
+                        h_ps[t, start][:, offset : offset + QUARTER], w4_t, ws34, W4_BASE, t, z2_words, z2_scales,
+                        cols, False, offset == QUARTER,
+                    )
 
-        h_sb = [sb(f"h_sb{t}", [P, S], F32) for t in range(PACK)]
-        for t in range(PACK):
-            if t % 2 == 0:
-                nc.scalar.activation(h_sb[t][:], h_ps[t][:], ACT.Copy)
-            else:
-                nc.vector.tensor_copy(h_sb[t][:], h_ps[t][:])
+        h_sb = [sb(f"h_sb{t}", [P, S], F32) for t in range(PLANES)]
+        for start in (0, HALF):
+            for t in range(PLANES):
+                if start == 0 or t % 2 == 0:
+                    nc.scalar.activation(h_sb[t][:, start : start + HALF], h_ps[t, start][:], ACT.Copy)
+                else:
+                    nc.vector.tensor_copy(h_sb[t][:, start : start + HALF], h_ps[t, start][:])
 
-        out_rows = out_0.rearrange("(p t) c -> p t c", t=PACK)
+        out_rows = out_0.rearrange("(p t) c -> p t c", t=PLANES)
         out_words = out_1[0].rearrange("p c t -> p (c t)").bitcast(I32)
-        o_bf = sb("o_bf", [P, S, PACK], BF16)
+        o_bf = sb("o_bf", [P, S, PLANES], BF16)
         o_words = sb("o_words", [P, S], I32)
         o_scales = sb("o_scales", [P, S], U8)
-        starts = [sum(OUT_CHUNKS[:c]) for c in range(len(OUT_CHUNKS))]
-        at3 = sb("at3", [P, PACK, S], F32)
-        first = sb("first", [P, PACK, S], F32)
-        def first_product(t, start):
-            both = slice(start, start + HALF)
-            fetch((t, start) not in N3_ON_VECTOR, at3[:, t, both], h_sb[t], n3_t, start, HALF)
-            nc.vector.scalar_tensor_tensor(first[:, t, both], h_ps[t][:, both], 0.75, at3[:, t, both], ALU.mult, ALU.mult)
+        h_at3 = sb("h_at3", [P, PLANES, S], F32)
+        h_at5 = sb("h_at5", [P, PLANES, OUT_CHUNKS[-1]], F32)
+        first = sb("first", [P, PLANES, S], F32)
 
-        for t, start in N3_ON_VECTOR:
-            first_product(t, start)
+        def first_term(on_scalar, t, start):
+            half = slice(start, start + HALF)
+            fetch(on_scalar, h_at3[:, t, half], h_sb[t], n3_t, start, HALF)
+            nc.vector.scalar_tensor_tensor(
+                first[:, t, half], h_ps[t, start][:], 0.75, h_at3[:, t, half], ALU.mult, ALU.mult
+            )
+
+        first_term(False, N3_PLANE_ON_VECTOR, 0)
         for c, width in enumerate(OUT_CHUNKS):
-            start = starts[c]
+            start = sum(OUT_CHUNKS[:c])
             cols = slice(start, start + width)
-            at4 = sb(f"at4_{c}", [P, PACK, width], F32)
-            second = sb(f"second{c}", [P, PACK, width], F32)
-            result = sb(f"result{c}", [P, PACK, width], F32)
-            for t in range(PACK):
-                fetch(True, at4[:, t, :], h_sb[t], n4_t, start, width)
-                nc.vector.tensor_tensor(
-                    second[:, t, :], h_sb[t][:].indirect(entries(n5_t, start, width)), at4[:, t, :], ALU.mult
-                )
+            h_at4 = sb(f"h_at4_{c}", [P, PLANES, width], F32)
+            second = sb(f"second{c}", [P, PLANES, width], F32)
+            result = sb(f"result{c}", [P, PLANES, width], F32)
+            for t in range(PLANES):
+                fetch(True, h_at4[:, t, :], h_sb[t], n4_t, start, width)
+                if c == len(OUT_CHUNKS) - 1 and t < N5_PLANES_ON_SCALAR:
+                    fetch(True, h_at5[:, t, :], h_sb[t], n5_t, start, width)
+                    factor = h_at5[:, t, :]
+                else:
+                    factor = h_sb[t][:].indirect(entries(n5_t, start, width))
+                nc.vector.tensor_tensor(second[:, t, :], factor, h_at4[:, t, :], ALU.mult)
             if start % HALF == 0:
-                for t in range(PACK):
-                    if (t, start) not in N3_ON_VECTOR:
-                        first_product(t, start)
+                for t in range(PLANES):
+                    if (t, start) != (N3_PLANE_ON_VECTOR, 0):
+                        first_term(True, t, start)
             nc.vector.scalar_tensor_tensor(result[:], second[:], 0.75, first[:, :, cols], ALU.mult, ALU.add)
             nc.sync.dma_start(out_rows[:, :, cols], result[:])
-            nc.vector.tensor_copy(woven(o_bf[:, cols, :]), planar(result[:]))
+            if c == CHUNK_WOVEN_ON_SCALAR:
+                nc.scalar.copy(woven(o_bf[:, cols, :]), planar(result[:]))
+            else:
+                nc.vector.tensor_copy(woven(o_bf[:, cols, :]), planar(result[:]))
             quantise(o_words, o_scales, o_bf, cols)
             nc.sync.dma_start(out_words[:, cols], o_words[:, cols])
-        for q in range(4):
+
+        for q in range(QUADRANTS):
             queue = nc.scalar if q % 2 == 0 else nc.sync
-            queue.dma_start(out_2[0, 4 * q : 4 * q + 4, :].bitcast(I32), o_scales[32 * q : 32 * q + 4, :].bitcast(I32))
+            queue.dma_start(
+                out_2[0, 4 * q : 4 * q + 4, :].bitcast(I32), o_scales[32 * q : 32 * q + 4, :].bitcast(I32)
+            )

from contextlib import ExitStack

import concourse.mybir as mybir
from concourse.masks import make_identity

T, S, H, N = 2048, 512, 512, 512
FLOPS = 4 * 2 * 512 * 512 * 512

F32 = mybir.dt.float32
BF16 = mybir.dt.bfloat16
I32 = mybir.dt.int32
U32 = mybir.dt.uint32
U16 = mybir.dt.uint16
U8 = mybir.dt.uint8
FP8X4 = mybir.dt.float8_e4m3fn_x4
ACT = mybir.ActivationFunctionType
ALU = mybir.AluOpType

P = 128
PLANES = 4
QUADRANTS = 4
QUARTERS = 4
QUARTER = S // QUARTERS
HALF = S // 2
W3_BASE, W4_BASE = 4, 8

OUT_CHUNKS = (HALF, QUARTER, QUARTER)
N3_PLANE_ON_VECTOR = 1
N5_PLANES_ON_SCALAR = 2
CHUNK_WOVEN_ON_SCALAR = 1


def tile_picked_hjoinharmnormdot_none_po_kernel(
    tc, x_words, x_scales, w1_words, w1_scales, w2_words, w2_scales, gn, gm,
    w3_words, w3_scales, w4_words, w4_scales, offs, hz, n1, n2, n3, n4, n5,
    out_0, out_1, out_2,
):
    nc = tc.nc

    with ExitStack() as ctx:
        keep = ctx.enter_context(tc.tile_pool(name="keep", bufs=1))
        psum = ctx.enter_context(tc.psum_pool(name="psum", bufs=1))

        def sb(name, shape, dtype, tag=None):
            return keep.tile(shape, dtype, name=name, tag=tag or name, align_bytes=64)

        def load_list(name, src):
            tile = keep.tile([P, S // 16], U16, name=name)
            nc.sync.dma_start(tile[:], src)
            return tile

        def load_words(tile, src):
            nc.sync.dma_start(tile[:], src[0].rearrange("p n t -> p (n t)").bitcast(I32))

        def load_scale_rows(queue, tile, src, base):
            for q in range(QUADRANTS):
                queue.dma_start(
                    tile[32 * q + base : 32 * q + base + 4, :].bitcast(I32),
                    src[0, 4 * q : 4 * q + 4, :].bitcast(I32),
                )

        def place_scale_rows(dst, picked):
            for r in range(4):
                nc.sync.dma_start(dst[r:P:32, :].bitcast(I32), picked[8 * r : P : 32, :].bitcast(I32))

        def deal(engine, name, raw, dtype, view):
            tile = sb(name, [P, H], dtype)
            engine.tensor_copy(
                tile[:].bitcast(view).rearrange("p (t m) -> p m t", t=PLANES),
                raw[:].bitcast(view).rearrange("p (m t) -> p m t", t=PLANES),
            )
            return tile

        def entries(lst, start, count):
            return lst[:, start // 16 : (start + count) // 16]

        def fetch(on_scalar, dst, window, lst, start, count):
            picked = window[:].indirect(entries(lst, start, count))
            if on_scalar:
                nc.scalar.activation(dst, picked, ACT.Copy)
            else:
                nc.vector.tensor_copy(dst, picked)

        def woven(ap):
            return ap.rearrange("p (c i) t -> p c t i", i=4)

        def planar(ap):
            return ap.rearrange("p t (c i) -> p c t i", i=4)

        def quantise(words, scales, values, cols):
            nc.vector.quantize_mx(
                out=words[:, cols].bitcast(FP8X4), scales=scales[:, cols],
                in_=values[:, cols, :].rearrange("p c t -> p (c t)"),
            )

        def product(out, words, scales, base, t, moving_words, moving_scales, cols, start, stop):
            m = slice(P * t, P * (t + 1))
            nc.tensor.matmul_mx(
                out=out, lhsT=words[:, m].bitcast(FP8X4), lhsT_scale=scales[base:P, m],
                rhs=moving_words[:, cols].bitcast(FP8X4), rhs_scale=moving_scales[:, cols],
                start=start, stop=stop,
            )

        def quarter_columns(j):
            return slice(QUARTER * j, QUARTER * (j + 1))

        all_columns = slice(0, S)

        xs_table = sb("xs_table", [P, T], U8)
        ws134_raw = sb("ws134_raw", [P, H], U8)
        ws2_raw = sb("ws2_raw", [P, H], U8)
        xs_offs = sb("xs_offs", [P, S], U8)
        xs_hz = sb("xs_hz", [P, S], U8)
        one_quarter = sb("one_quarter", [P, 1], F32)
        one_half = sb("one_half", [P, 1], F32)
        nc.gpsimd.memset(xs_table[:].bitcast(I32), 0)
        nc.gpsimd.memset(ws134_raw[:].bitcast(I32), 0)
        nc.gpsimd.memset(ws2_raw[:].bitcast(I32), 0)
        nc.gpsimd.memset(one_half[:], 0.5)
        for tile in (xs_offs, xs_hz):
            nc.vector.memset(tile[:].bitcast(I32), 0)
        nc.vector.memset(one_quarter[:], 0.25)

        xw_table = sb("xw_table", [P, T], I32)
        w1_raw = sb("w1_raw", [P, H], I32)
        w24_raw = sb("w24_raw", [P, H], I32)
        gn_t = sb("gn_t", [P, PLANES], F32)
        gm_t = sb("gm_t", [P, PLANES], F32)
        offs_t = load_list("offs_t", offs)
        nc.sync.dma_start(xs_table[0:P:8, :].bitcast(I32), x_scales[0].bitcast(I32))
        load_scale_rows(nc.scalar, ws134_raw, w1_scales, 0)
        hz_t = load_list("hz_t", hz)
        load_words(xw_table, x_words)
        load_words(w1_raw, w1_words)
        load_scale_rows(nc.gpsimd, ws2_raw, w2_scales, 0)

        warm = sb("warm", [P, 1], F32)
        nc.scalar.activation(warm[:], one_half[:], ACT.Abs_reciprocal_sqrt)

        picked_offs = sb("picked_offs", [P, S], U8)
        picked_hz = sb("picked_hz", [P, S], U8)
        nc.vector.tensor_copy(picked_offs[:], xs_table[:].indirect(offs_t[:]))
        place_scale_rows(xs_offs, picked_offs)
        nc.vector.tensor_copy(picked_hz[:], xs_table[:].indirect(hz_t[:]))
        ws1 = deal(nc.vector, "ws1", ws134_raw, U8, U8)
        w1_t = deal(nc.vector, "w1_t", w1_raw, I32, U32)
        n1_t = load_list("n1_t", n1)
        load_words(w24_raw, w2_words)

        xw_offs = sb("xw_offs", [P, S], I32)
        nc.vector.tensor_copy(xw_offs[:].bitcast(U32), xw_table[:].bitcast(U32).indirect(offs_t[:]))
        y_ps = [psum.tile([P, S], F32, name=f"y_ps{t}", tag=f"plane{t}") for t in range(PLANES)]
        for t in range(PLANES):
            product(y_ps[t][:], w1_t, ws1, 0, t, xw_offs, xs_offs, all_columns, True, True)

        place_scale_rows(xs_hz, picked_hz)
        nc.sync.dma_start(gn_t[:], gn.rearrange("(p t) o -> p (t o)", t=PLANES))
        nc.sync.dma_start(gm_t[:], gm.rearrange("(p t) o -> p (t o)", t=PLANES))
        n2_t = load_list("n2_t", n2)
        xw_hz = sb("xw_hz", [P, S], I32, tag="w1_raw")
        nc.vector.tensor_copy(xw_hz[:].bitcast(U32), xw_table[:].bitcast(U32).indirect(hz_t[:]))

        y_sb = [sb(f"y_sb{t}", [P, S], F32) for t in range(PLANES)]
        y_sq = sb("y_sq", [P, PLANES, S], F32)
        pa = sb("pa", [P, PLANES, S], F32)
        pa_sq = sb("pa_sq", [P, PLANES, S], F32)
        y_root = [sb(f"y_root{j}", [P, H], F32) for j in range(QUARTERS)]
        numer = sb("numer", [P, PLANES, S], F32)
        inverse = [sb(f"inverse{j}", [P, H], F32) for j in range(QUARTERS)]
        z_bf = sb("z_bf", [P, S, PLANES], BF16)
        z_words = sb("z_words", [P, S], U32)
        z_scales = sb("z_scales", [P, S], U8)
        d_abs = [sb(f"d_abs{j}", [P, PLANES * QUARTER], F32) for j in range(QUARTERS)]
        d_root = sb("d_root", [P, QUARTERS, PLANES, QUARTER], F32)
        gain_over = [sb(f"gain_over{t}", [P, S], F32) for t in range(PLANES)]
        gain_at2 = sb("gain_at2", [P, PLANES, S], F32)
        z2_bf = sb("z2_bf", [P, S, PLANES], BF16)
        z2_words = sb("z2_words", [P, S], U32)
        z2_scales = sb("z2_scales", [P, S], U8)

        for t in range(PLANES):
            nc.scalar.activation(y_sb[t][:], y_ps[t][:], ACT.Copy)

        identity = sb("identity", [P, P], F32)
        make_identity(nc, identity[:])

        w2_t = deal(nc.vector, "w2_t", w24_raw, I32, U32)
        ws2 = deal(nc.gpsimd, "ws2", ws2_raw, U8, U8)
        w3_raw = sb("w3_raw", [P, N], I32, tag="xw_offs")
        load_words(w3_raw, w3_words)
        load_words(w24_raw, w4_words)
        load_scale_rows(nc.sync, ws134_raw, w3_scales, W3_BASE)
        load_scale_rows(nc.sync, ws134_raw, w4_scales, W4_BASE)
        n3_t = load_list("n3_t", n3)
        n4_t = load_list("n4_t", n4)
        n5_t = load_list("n5_t", n5)

        d_ps = [psum.tile([P, PLANES, QUARTER], F32, name=f"d_ps{j}", tag=f"quarter{j}") for j in range(QUARTERS)]
        for j in range(QUARTERS):
            for t in range(PLANES):
                product(d_ps[j][:, t, :], w2_t, ws2, 0, t, xw_hz, xs_hz, quarter_columns(j), True, True)

        for t in range(PLANES):
            nc.scalar.activation(y_sq[:, t, :], y_ps[t][:], ACT.Square)
        for start in (0, HALF):
            for t in range(PLANES):
                fetch(False, pa[:, t, start : start + HALF], y_sb[t], n1_t, start, HALF)

        for j in range(QUARTERS):
            nc.scalar.activation(d_abs[j][:], d_ps[j][:].rearrange("p t c -> p (t c)"), ACT.Abs)
        for j in range(QUARTERS):
            nc.scalar.activation(
                d_root[:, j, :, :].rearrange("p t c -> p (t c)"), d_abs[j][:],
                ACT.Abs_reciprocal_sqrt, bias=one_half[:], scale=1.0,
            )

        for j in range(QUARTERS):
            cols = quarter_columns(j)
            nc.vector.tensor_tensor(pa_sq[:, :, cols], pa[:, :, cols], pa[:, :, cols], ALU.mult)
        for t in range(PLANES):
            nc.vector.scalar_tensor_tensor(
                numer[:, t, :], y_sb[t][:], gn_t[:, t : t + 1], pa[:, t, :], ALU.mult, ALU.mult
            )

        for t in range(PLANES):
            nc.vector.scalar_tensor_tensor(
                gain_over[t][:].rearrange("p (j c) -> p j c", j=QUARTERS), d_root[:, :, t, :],
                gm_t[:, t : t + 1], d_root[:, :, t, :], ALU.mult, ALU.mult,
            )
        w3_t = deal(nc.vector, "w3_t", w3_raw, I32, U32)
        w4_t = deal(nc.vector, "w4_t", w24_raw, I32, U32)
        ws34 = deal(nc.vector, "ws34", ws134_raw, U8, U8)

        squares_ps = [psum.tile([P, PLANES, P], F32, name=f"squares_ps{j}", tag=f"plane{j}") for j in range(QUARTERS)]
        for term, is_first in ((y_sq, True), (pa_sq, False)):
            for j in range(QUARTERS):
                for t in range(PLANES):
                    nc.tensor.matmul(
                        squares_ps[j][:, t, :], lhsT=term[:, t, quarter_columns(j)], rhs=identity[:],
                        start=is_first and t == 0, stop=not is_first and t == PLANES - 1, is_transpose=True,
                    )

        for j in range(QUARTERS):
            cols = quarter_columns(j)
            nc.scalar.activation(
                y_root[j][:], squares_ps[j][:].rearrange("c t p -> c (t p)"),
                ACT.Abs_reciprocal_sqrt, bias=one_quarter[:], scale=0.5,
            )
            nc.scalar.activation(inverse[j][:], y_root[j][:], ACT.Square)
            inverse_ps = psum.tile([P, PLANES, QUARTER], F32, name=f"inverse_ps{j}", tag=f"plane{j}")
            for t in range(PLANES):
                nc.tensor.transpose(inverse_ps[:, t, :], inverse[j][:, P * t : P * (t + 1)], identity[:])
            nc.vector.tensor_tensor(
                woven(z_bf[:, cols, :]), planar(inverse_ps[:]), planar(numer[:, :, cols]), ALU.mult
            )
            quantise(z_words, z_scales, z_bf, cols)

        for j in range(QUARTERS):
            cols = quarter_columns(j)
            for t in range(PLANES):
                fetch(True, gain_at2[:, t, cols], gain_over[t], n2_t, cols.start, QUARTER)
            nc.vector.tensor_tensor(
                woven(z2_bf[:, cols, :]), planar(d_ps[j][:]), planar(gain_at2[:, :, cols]), ALU.mult
            )
            quantise(z2_words, z2_scales, z2_bf, cols)

        h_ps = {}
        for start, banks in ((0, "plane"), (HALF, "quarter")):
            for t in range(PLANES):
                h_ps[t, start] = psum.tile([P, HALF], F32, name=f"h_ps{t}_{start}", tag=f"{banks}{t}")
                product(
                    h_ps[t, start][:], w3_t, ws34, W3_BASE, t, z_words, z_scales,
                    slice(start, start + HALF), True, False,
                )
            for offset in (0, QUARTER):
                cols = slice(start + offset, start + offset + QUARTER)
                for t in range(PLANES):
                    product(
                        h_ps[t, start][:, offset : offset + QUARTER], w4_t, ws34, W4_BASE, t, z2_words, z2_scales,
                        cols, False, offset == QUARTER,
                    )

        h_sb = [sb(f"h_sb{t}", [P, S], F32) for t in range(PLANES)]
        for start in (0, HALF):
            for t in range(PLANES):
                if start == 0 or t % 2 == 0:
                    nc.scalar.activation(h_sb[t][:, start : start + HALF], h_ps[t, start][:], ACT.Copy)
                else:
                    nc.vector.tensor_copy(h_sb[t][:, start : start + HALF], h_ps[t, start][:])

        out_rows = out_0.rearrange("(p t) c -> p t c", t=PLANES)
        out_words = out_1[0].rearrange("p c t -> p (c t)").bitcast(I32)
        o_bf = sb("o_bf", [P, S, PLANES], BF16)
        o_words = sb("o_words", [P, S], I32)
        o_scales = sb("o_scales", [P, S], U8)
        h_at3 = sb("h_at3", [P, PLANES, S], F32)
        h_at5 = sb("h_at5", [P, PLANES, OUT_CHUNKS[-1]], F32)
        first = sb("first", [P, PLANES, S], F32)

        def first_term(on_scalar, t, start):
            half = slice(start, start + HALF)
            fetch(on_scalar, h_at3[:, t, half], h_sb[t], n3_t, start, HALF)
            nc.vector.scalar_tensor_tensor(
                first[:, t, half], h_ps[t, start][:], 0.75, h_at3[:, t, half], ALU.mult, ALU.mult
            )

        first_term(False, N3_PLANE_ON_VECTOR, 0)
        for c, width in enumerate(OUT_CHUNKS):
            start = sum(OUT_CHUNKS[:c])
            cols = slice(start, start + width)
            h_at4 = sb(f"h_at4_{c}", [P, PLANES, width], F32)
            second = sb(f"second{c}", [P, PLANES, width], F32)
            result = sb(f"result{c}", [P, PLANES, width], F32)
            for t in range(PLANES):
                fetch(True, h_at4[:, t, :], h_sb[t], n4_t, start, width)
                if c == len(OUT_CHUNKS) - 1 and t < N5_PLANES_ON_SCALAR:
                    fetch(True, h_at5[:, t, :], h_sb[t], n5_t, start, width)
                    factor = h_at5[:, t, :]
                else:
                    factor = h_sb[t][:].indirect(entries(n5_t, start, width))
                nc.vector.tensor_tensor(second[:, t, :], factor, h_at4[:, t, :], ALU.mult)
            if start % HALF == 0:
                for t in range(PLANES):
                    if (t, start) != (N3_PLANE_ON_VECTOR, 0):
                        first_term(True, t, start)
            nc.vector.scalar_tensor_tensor(result[:], second[:], 0.75, first[:, :, cols], ALU.mult, ALU.add)
            nc.sync.dma_start(out_rows[:, :, cols], result[:])
            if c == CHUNK_WOVEN_ON_SCALAR:
                nc.scalar.copy(woven(o_bf[:, cols, :]), planar(result[:]))
            else:
                nc.vector.tensor_copy(woven(o_bf[:, cols, :]), planar(result[:]))
            quantise(o_words, o_scales, o_bf, cols)
            nc.sync.dma_start(out_words[:, cols], o_words[:, cols])

        for q in range(QUADRANTS):
            queue = nc.scalar if q % 2 == 0 else nc.sync
            queue.dma_start(
                out_2[0, 4 * q : 4 * q + 4, :].bitcast(I32), o_scales[32 * q : 32 * q + 4, :].bitcast(I32)
            )
